import numpy as np
import ml_dtypes


def mxq(x, axis, fmt="e4m3"):
    dtype, down = {"e4m3": (ml_dtypes.float8_e4m3fn, 7), "e5m2": (ml_dtypes.float8_e5m2, 14)}[fmt]
    v = np.moveaxis(np.asarray(x, np.float32).astype(ml_dtypes.bfloat16).astype(np.float64), axis, -1)
    blocks = v.reshape(v.shape[:-1] + (-1, 32))
    amax = np.abs(blocks).max(-1, keepdims=True)
    byte = np.maximum(np.where(amax > 0, np.frexp(amax)[1] - 1 + 127, 0) - down, 1)
    scale = np.exp2(byte - 127.0)
    codes = (blocks / scale).astype(np.float32).astype(dtype).astype(np.float64)
    return np.moveaxis((codes * scale).reshape(v.shape), -1, axis)


WIDE = False


def mx_kscale(k):
    if not WIDE:
        return np.ones(k)
    levels = np.array([10, -10, 5, -5, 0])
    if k % 512:
        return np.exp2(np.random.permutation(np.resize(levels, k // 32))).repeat(32)
    a = np.empty((k // 512, 16))
    for p in range(k // 512):
        a[p, :8] = np.random.permutation(np.resize(levels, 8))
        for g in range(8):
            far = levels[np.abs(levels - a[p, g]) >= 10]
            a[p, g + 8] = far[np.random.randint(len(far))]
    return np.exp2(a.ravel()).repeat(32)


def f64(x):
    return np.asarray(x).astype(np.float64)


def striped(idx):
    return np.tile(idx.reshape(-1, 16).T, (8, 1)).astype(np.uint16)


def unstriped(offs):
    return offs[:16].T.reshape(-1).astype(np.int64)


K, T, S, N = 512, 2048, 512, 256


def setup_inputs():
    n = np.random.standard_normal
    s = mx_kscale(K)[:, None]
    return {
        "xT": (n((K, T)) * s).astype(np.float32),
        "w1": (n((K, N)) / np.sqrt(3 * K) / s).astype(np.float32),
        "w2": (n((K, N)) / np.sqrt(3 * K) / s).astype(np.float32),
        "w3": (n((K, N)) / np.sqrt(3 * K) / s).astype(np.float32),
        "offs": striped(np.random.permutation(T)[:S]),
    }


def reference(xT, w1, w2, w3, offs):
    xq = mxq(f64(xT)[:, unstriped(offs)], 0, "e4m3")
    y0 = mxq(f64(w1), 0, "e4m3").T @ xq
    y1 = mxq(f64(w2), 0, "e4m3").T @ xq
    y2 = mxq(f64(w3), 0, "e4m3").T @ xq
    return y0 + np.pad(y1, ((0, 0), (1, 0)))[:, :S] + np.pad(y2, ((0, 0), (2, 0)))[:, :S]

@@ -1,0 +1,129 @@
+from contextlib import ExitStack
+
+import concourse.mybir as mybir
+
+K, T, S, N = 512, 2048, 512, 256
+TAPS = 3
+FLOPS = 2 * TAPS * K * N * S
+
+F32 = mybir.dt.float32
+BF16 = mybir.dt.bfloat16
+U32 = mybir.dt.uint32
+U16 = mybir.dt.uint16
+U8 = mybir.dt.uint8
+FP8X4 = mybir.dt.float8_e4m3fn_x4
+
+P = 128
+PACK = 4
+PHASES = 4
+RUN = S // PHASES
+LEAD = (TAPS - 1) * RUN
+BLOCKS = N // P
+WARM_ROWS = 32
+WARM_PASSES = 0
+
+
+def tile_picked_listconv_none_e_kernel(tc, xT, w1, w2, w3, offs, out):
+    nc = tc.nc
+    with ExitStack() as ctx:
+        keep = ctx.enter_context(tc.tile_pool(name="keep", bufs=1))
+        psum = ctx.enter_context(tc.psum_pool(name="psum", bufs=1))
+
+        offsets = keep.tile([P, S // 16], U16, name="offsets")
+        x_rows = xT.rearrange("(p t) n -> p t n", t=PACK)
+        planes = []
+        for t in range(PACK):
+            plane = keep.tile([P, T], F32, name="plane%d" % t, align_bytes=64)
+            nc.sync.dma_start(out=plane[:], in_=x_rows[:, t, :])
+            planes.append(plane)
+            if t == 0:
+                nc.sync.dma_start(offsets[:], offs)
+        raws = []
+        for d, w in enumerate((w1, w2, w3)):
+            raw = keep.tile([P, PACK, N], F32, name="raw%d" % d, align_bytes=64)
+            nc.sync.dma_start(out=raw[:], in_=w.rearrange("(p t) c -> p t c", t=PACK))
+            raws.append(raw)
+
+        x_codes = keep.tile([P, LEAD + S], U32, name="x_codes", align_bytes=64)
+        x_scales = keep.tile([P, LEAD + S], U8, name="x_scales", align_bytes=64)
+        nc.vector.memset(x_codes[:, 0:LEAD], 0)
+        nc.vector.memset(x_scales[:], 0)
+
+        picked = keep.tile([P, S * PACK], BF16, name="picked", align_bytes=64)
+        picked_by_entry = picked[:].rearrange("p (r i t) -> p i r t", r=PHASES, t=PACK)
+
+        def gather(t, first, count):
+            nc.vector.tensor_copy(
+                out=picked_by_entry[:, first // PHASES : (first + count) // PHASES, :, t],
+                in_=planes[t][:].indirect(offsets[:, first // 16 : (first + count) // 16]),
+            )
+
+        gather(0, 0, S)
+        gather(1, 0, S)
+        gather(2, 0, S)
+        gather(3, 0, S)
+
+        for first in (S // 2, 0):
+            cols = slice(LEAD + first, LEAD + first + S // 2)
+            nc.vector.quantize_mx(
+                out=x_codes[:, cols].bitcast(FP8X4),
+                scales=x_scales[:, cols],
+                in_=picked[:, first * PACK : (first + S // 2) * PACK],
+            )
+
+        def shift(whole):
+            nc.vector.tensor_copy(
+                out=whole[:, 0:LEAD].rearrange("p (r i) -> p r i", i=RUN)[:, :, 1:RUN],
+                in_=whole[:, S : S + LEAD].rearrange("p (r i) -> p r i", i=RUN)[:, :, 0 : RUN - 1],
+            )
+
+        def prepare(d, b, copy, scales):
+            cols = slice(b * P, (b + 1) * P)
+            tag = "grouped01" if (d, b) == (TAPS - 1, 0) else "grouped%d%d" % (d, b)
+            grouped = keep.tile([P, P, PACK], BF16, name="grouped%d%d" % (d, b), tag=tag, align_bytes=64)
+            copy(
+                out=grouped[:].rearrange("p (c i) t -> p c t i", i=4),
+                in_=raws[d][:, :, cols].rearrange("p t (c i) -> p c t i", i=4),
+            )
+            codes = keep.tile([P, P], U32, name="w_codes%d%d" % (d, b), align_bytes=64)
+            nc.vector.quantize_mx(
+                out=codes[:].bitcast(FP8X4), scales=scales, in_=grouped[:].rearrange("p c t -> p (c t)")
+            )
+            return codes, scales
+
+        weights = {}
+        shift(x_codes)
+        for d in range(TAPS):
+            for b in range(BLOCKS):
+                copy = nc.vector.tensor_copy if (d, b) == (TAPS - 1, 0) else nc.scalar.copy
+                if (d, b) == (0, 0):
+                    scales = x_scales[4:P, S : S + P]
+                else:
+                    own = keep.tile([P, P], U8, name="w_scales%d%d" % (d, b), align_bytes=64)
+                    scales = own[:]
+                weights[(d, b)] = prepare(d, b, copy, scales)
+            if d == 0:
+                shift(x_scales)
+
+        sums = [psum.tile([P, S], F32, name="sums%d" % b) for b in range(BLOCKS)]
+        for d, b in ((0, 0), (0, 1), (1, 0), (2, 0), (1, 1), (2, 1)):
+            codes, scales = weights[(d, b)]
+            first = LEAD - d * RUN
+            nc.tensor.matmul_mx(
+                out=sums[b][:],
+                lhsT=codes[:].bitcast(FP8X4),
+                lhsT_scale=scales,
+                rhs=x_codes[:, first : first + S].bitcast(FP8X4),
+                rhs_scale=x_scales[:, first : first + S],
+                start=(d == 0),
+                stop=(d == TAPS - 1),
+            )
+
+        for b in range(BLOCKS):
+            result = keep.tile([P, S], F32, name="result%d" % b)
+            copy = nc.scalar.copy if b == 0 else nc.vector.tensor_copy
+            copy(
+                out=result[:].rearrange("p (i r) -> p i r", r=PHASES),
+                in_=sums[b][:].rearrange("p (r i) -> p i r", r=PHASES),
+            )
+            nc.sync.dma_start(out=out[b * P : (b + 1) * P, :], in_=result[:])

@@ -20,7 +20,7 @@ RUN = S // PHASES
 LEAD = (TAPS - 1) * RUN
 BLOCKS = N // P
 WARM_ROWS = 32
-WARM_PASSES = 0
+WARM_PASSES = 24
 
 
 def tile_picked_listconv_none_e_kernel(tc, xT, w1, w2, w3, offs, out):
@@ -58,9 +58,30 @@ def tile_picked_listconv_none_e_kernel(tc, xT, w1, w2, w3, offs, out):
                 in_=planes[t][:].indirect(offsets[:, first // 16 : (first + count) // 16]),
             )
 
+        nc.vector.memset(picked[:, 0 : RUN * PACK], 0.0)
         gather(0, 0, S)
         gather(1, 0, S)
-        gather(2, 0, S)
+        warm_codes = keep.tile([P, RUN], U32, name="warm_codes", align_bytes=64)
+        warm_scales = keep.tile([P, RUN], U8, name="warm_scales", align_bytes=64)
+        nc.vector.quantize_mx(out=warm_codes[:].bitcast(FP8X4), scales=warm_scales[:], in_=picked[:, 0 : RUN * PACK])
+        gather(2, 0, S // 2)
+        gather(2, S // 2, S // 2)
+        cue_codes = keep.tile([P, WARM_ROWS], U32, name="cue_codes", align_bytes=64)
+        cue_scales = keep.tile([P, WARM_ROWS], U8, name="cue_scales", align_bytes=64)
+        nc.vector.quantize_mx(
+            out=cue_codes[:].bitcast(FP8X4), scales=cue_scales[:], in_=picked[:, 0 : WARM_ROWS * PACK]
+        )
+        warm_sums = psum.tile([WARM_ROWS, S], F32, name="warm_sums")
+        for n in range(WARM_PASSES):
+            nc.tensor.matmul_mx(
+                out=warm_sums[:, (n % PHASES) * RUN : (n % PHASES + 1) * RUN],
+                lhsT=cue_codes[:].bitcast(FP8X4),
+                lhsT_scale=cue_scales[:],
+                rhs=warm_codes[:].bitcast(FP8X4),
+                rhs_scale=warm_scales[:],
+                start=True,
+                stop=True,
+            )
         gather(3, 0, S)
 
         for first in (S // 2, 0):

@@ -21,6 +21,9 @@ LEAD = (TAPS - 1) * RUN
 BLOCKS = N // P
 WARM_ROWS = 32
 WARM_PASSES = 24
+EARLY = 192
+MID = 352
+LOAD_ORDER = (2, 0, 1, 3)
 
 
 def tile_picked_listconv_none_e_kernel(tc, xT, w1, w2, w3, offs, out):
@@ -31,12 +34,12 @@ def tile_picked_listconv_none_e_kernel(tc, xT, w1, w2, w3, offs, out):
 
         offsets = keep.tile([P, S // 16], U16, name="offsets")
         x_rows = xT.rearrange("(p t) n -> p t n", t=PACK)
-        planes = []
-        for t in range(PACK):
+        planes = {}
+        for t in LOAD_ORDER:
             plane = keep.tile([P, T], F32, name="plane%d" % t, align_bytes=64)
             nc.sync.dma_start(out=plane[:], in_=x_rows[:, t, :])
-            planes.append(plane)
-            if t == 0:
+            planes[t] = plane
+            if t == LOAD_ORDER[0]:
                 nc.sync.dma_start(offsets[:], offs)
         raws = []
         for d, w in enumerate((w1, w2, w3)):
@@ -50,39 +53,49 @@ def tile_picked_listconv_none_e_kernel(tc, xT, w1, w2, w3, offs, out):
         nc.vector.memset(x_scales[:], 0)
 
         picked = keep.tile([P, S * PACK], BF16, name="picked", align_bytes=64)
-        picked_by_entry = picked[:].rearrange("p (r i t) -> p i r t", r=PHASES, t=PACK)
+        picked_runs = picked[:].rearrange("p (r i t) -> p r i t", r=PHASES, t=PACK)
 
-        def gather(t, first, count):
-            nc.vector.tensor_copy(
-                out=picked_by_entry[:, first // PHASES : (first + count) // PHASES, :, t],
-                in_=planes[t][:].indirect(offsets[:, first // 16 : (first + count) // 16]),
-            )
+        def fetch(t):
+            dense = keep.tile([P, S], BF16, name="dense%d" % t, align_bytes=64)
+            cuts = (0, EARLY, S) if (t < 2 or MID == EARLY) else (0, EARLY, MID, S)
+            for first, last in zip(cuts[:-1], cuts[1:]):
+                nc.vector.tensor_copy(
+                    out=dense[:, first:last], in_=planes[t][:].indirect(offsets[:, first // 16 : last // 16])
+                )
+            dense_runs = dense[:].rearrange("p (i r) -> p r i", r=PHASES)
 
-        nc.vector.memset(picked[:, 0 : RUN * PACK], 0.0)
-        gather(0, 0, S)
-        gather(1, 0, S)
+            def insert(copy, runs, first, last):
+                places = slice(first // PHASES, last // PHASES)
+                copy(out=picked_runs[:, runs, places, t], in_=dense_runs[:, runs, places])
+
+            insert(nc.scalar.copy, slice(0, 4), 0, EARLY)
+            if t < 2:
+                insert(nc.scalar.copy, slice(0, 4), EARLY, S)
+            else:
+                if MID > EARLY:
+                    insert(nc.vector.tensor_copy, slice(0, 4), EARLY, MID)
+                for runs in (slice(2, 4), slice(0, 2)):
+                    insert(nc.vector.tensor_copy, runs, MID, S)
+            return dense
+
+        fetch(2)
+        fetch(0)
+        cue = fetch(1)
         warm_codes = keep.tile([P, RUN], U32, name="warm_codes", align_bytes=64)
         warm_scales = keep.tile([P, RUN], U8, name="warm_scales", align_bytes=64)
-        nc.vector.quantize_mx(out=warm_codes[:].bitcast(FP8X4), scales=warm_scales[:], in_=picked[:, 0 : RUN * PACK])
-        gather(2, 0, S // 2)
-        gather(2, S // 2, S // 2)
-        cue_codes = keep.tile([P, WARM_ROWS], U32, name="cue_codes", align_bytes=64)
-        cue_scales = keep.tile([P, WARM_ROWS], U8, name="cue_scales", align_bytes=64)
-        nc.vector.quantize_mx(
-            out=cue_codes[:].bitcast(FP8X4), scales=cue_scales[:], in_=picked[:, 0 : WARM_ROWS * PACK]
-        )
+        nc.vector.quantize_mx(out=warm_codes[:].bitcast(FP8X4), scales=warm_scales[:], in_=cue[:])
         warm_sums = psum.tile([WARM_ROWS, S], F32, name="warm_sums")
         for n in range(WARM_PASSES):
             nc.tensor.matmul_mx(
                 out=warm_sums[:, (n % PHASES) * RUN : (n % PHASES + 1) * RUN],
-                lhsT=cue_codes[:].bitcast(FP8X4),
-                lhsT_scale=cue_scales[:],
+                lhsT=warm_codes[:, 0:WARM_ROWS].bitcast(FP8X4),
+                lhsT_scale=warm_scales[:, 0:WARM_ROWS],
                 rhs=warm_codes[:].bitcast(FP8X4),
                 rhs_scale=warm_scales[:],
                 start=True,
                 stop=True,
             )
-        gather(3, 0, S)
+        fetch(3)
 
         for first in (S // 2, 0):
             cols = slice(LEAD + first, LEAD + first + S // 2)
@@ -114,17 +127,13 @@ def tile_picked_listconv_none_e_kernel(tc, xT, w1, w2, w3, offs, out):
 
         weights = {}
         shift(x_codes)
+        shift(x_scales)
         for d in range(TAPS):
             for b in range(BLOCKS):
                 copy = nc.vector.tensor_copy if (d, b) == (TAPS - 1, 0) else nc.scalar.copy
-                if (d, b) == (0, 0):
-                    scales = x_scales[4:P, S : S + P]
-                else:
-                    own = keep.tile([P, P], U8, name="w_scales%d%d" % (d, b), align_bytes=64)
-                    scales = own[:]
+                own = keep.tile([P, P], U8, name="w_scales%d%d" % (d, b), align_bytes=64)
+                scales = own[:]
                 weights[(d, b)] = prepare(d, b, copy, scales)
-            if d == 0:
-                shift(x_scales)
 
         sums = [psum.tile([P, S], F32, name="sums%d" % b) for b in range(BLOCKS)]
         for d, b in ((0, 0), (0, 1), (1, 0), (2, 0), (1, 1), (2, 1)):

from contextlib import ExitStack

import concourse.mybir as mybir

K, T, S, N = 512, 2048, 512, 256
TAPS = 3
FLOPS = 2 * TAPS * K * N * S

F32 = mybir.dt.float32
BF16 = mybir.dt.bfloat16
U32 = mybir.dt.uint32
U16 = mybir.dt.uint16
U8 = mybir.dt.uint8
FP8X4 = mybir.dt.float8_e4m3fn_x4

P = 128
PACK = 4
PHASES = 4
RUN = S // PHASES
LEAD = (TAPS - 1) * RUN
BLOCKS = N // P
WARM_ROWS = 32
WARM_PASSES = 24
EARLY = 192
MID = 352
LOAD_ORDER = (2, 0, 1, 3)


def tile_picked_listconv_none_e_kernel(tc, xT, w1, w2, w3, offs, out):
    nc = tc.nc
    with ExitStack() as ctx:
        keep = ctx.enter_context(tc.tile_pool(name="keep", bufs=1))
        psum = ctx.enter_context(tc.psum_pool(name="psum", bufs=1))

        offsets = keep.tile([P, S // 16], U16, name="offsets")
        x_rows = xT.rearrange("(p t) n -> p t n", t=PACK)
        planes = {}
        for t in LOAD_ORDER:
            plane = keep.tile([P, T], F32, name="plane%d" % t, align_bytes=64)
            nc.sync.dma_start(out=plane[:], in_=x_rows[:, t, :])
            planes[t] = plane
            if t == LOAD_ORDER[0]:
                nc.sync.dma_start(offsets[:], offs)
        raws = []
        for d, w in enumerate((w1, w2, w3)):
            raw = keep.tile([P, PACK, N], F32, name="raw%d" % d, align_bytes=64)
            nc.sync.dma_start(out=raw[:], in_=w.rearrange("(p t) c -> p t c", t=PACK))
            raws.append(raw)

        x_codes = keep.tile([P, LEAD + S], U32, name="x_codes", align_bytes=64)
        x_scales = keep.tile([P, LEAD + S], U8, name="x_scales", align_bytes=64)
        nc.vector.memset(x_codes[:, 0:LEAD], 0)
        nc.vector.memset(x_scales[:], 0)

        picked = keep.tile([P, S * PACK], BF16, name="picked", align_bytes=64)
        picked_runs = picked[:].rearrange("p (r i t) -> p r i t", r=PHASES, t=PACK)

        def fetch(t):
            dense = keep.tile([P, S], BF16, name="dense%d" % t, align_bytes=64)
            cuts = (0, EARLY, S) if (t < 2 or MID == EARLY) else (0, EARLY, MID, S)
            for first, last in zip(cuts[:-1], cuts[1:]):
                nc.vector.tensor_copy(
                    out=dense[:, first:last], in_=planes[t][:].indirect(offsets[:, first // 16 : last // 16])
                )
            dense_runs = dense[:].rearrange("p (i r) -> p r i", r=PHASES)

            def insert(copy, runs, first, last):
                places = slice(first // PHASES, last // PHASES)
                copy(out=picked_runs[:, runs, places, t], in_=dense_runs[:, runs, places])

            insert(nc.scalar.copy, slice(0, 4), 0, EARLY)
            if t < 2:
                insert(nc.scalar.copy, slice(0, 4), EARLY, S)
            else:
                if MID > EARLY:
                    insert(nc.vector.tensor_copy, slice(0, 4), EARLY, MID)
                for runs in (slice(2, 4), slice(0, 2)):
                    insert(nc.vector.tensor_copy, runs, MID, S)
            return dense

        fetch(2)
        fetch(0)
        cue = fetch(1)
        warm_codes = keep.tile([P, RUN], U32, name="warm_codes", align_bytes=64)
        warm_scales = keep.tile([P, RUN], U8, name="warm_scales", align_bytes=64)
        nc.vector.quantize_mx(out=warm_codes[:].bitcast(FP8X4), scales=warm_scales[:], in_=cue[:])
        warm_sums = psum.tile([WARM_ROWS, S], F32, name="warm_sums")
        for n in range(WARM_PASSES):
            nc.tensor.matmul_mx(
                out=warm_sums[:, (n % PHASES) * RUN : (n % PHASES + 1) * RUN],
                lhsT=warm_codes[:, 0:WARM_ROWS].bitcast(FP8X4),
                lhsT_scale=warm_scales[:, 0:WARM_ROWS],
                rhs=warm_codes[:].bitcast(FP8X4),
                rhs_scale=warm_scales[:],
                start=True,
                stop=True,
            )
        fetch(3)

        for first in (S // 2, 0):
            cols = slice(LEAD + first, LEAD + first + S // 2)
            nc.vector.quantize_mx(
                out=x_codes[:, cols].bitcast(FP8X4),
                scales=x_scales[:, cols],
                in_=picked[:, first * PACK : (first + S // 2) * PACK],
            )

        def shift(whole):
            nc.vector.tensor_copy(
                out=whole[:, 0:LEAD].rearrange("p (r i) -> p r i", i=RUN)[:, :, 1:RUN],
                in_=whole[:, S : S + LEAD].rearrange("p (r i) -> p r i", i=RUN)[:, :, 0 : RUN - 1],
            )

        def prepare(d, b, copy, scales):
            cols = slice(b * P, (b + 1) * P)
            tag = "grouped01" if (d, b) == (TAPS - 1, 0) else "grouped%d%d" % (d, b)
            grouped = keep.tile([P, P, PACK], BF16, name="grouped%d%d" % (d, b), tag=tag, align_bytes=64)
            copy(
                out=grouped[:].rearrange("p (c i) t -> p c t i", i=4),
                in_=raws[d][:, :, cols].rearrange("p t (c i) -> p c t i", i=4),
            )
            codes = keep.tile([P, P], U32, name="w_codes%d%d" % (d, b), align_bytes=64)
            nc.vector.quantize_mx(
                out=codes[:].bitcast(FP8X4), scales=scales, in_=grouped[:].rearrange("p c t -> p (c t)")
            )
            return codes, scales

        weights = {}
        shift(x_codes)
        shift(x_scales)
        for d in range(TAPS):
            for b in range(BLOCKS):
                copy = nc.vector.tensor_copy if (d, b) == (TAPS - 1, 0) else nc.scalar.copy
                own = keep.tile([P, P], U8, name="w_scales%d%d" % (d, b), align_bytes=64)
                scales = own[:]
                weights[(d, b)] = prepare(d, b, copy, scales)

        sums = [psum.tile([P, S], F32, name="sums%d" % b) for b in range(BLOCKS)]
        for d, b in ((0, 0), (0, 1), (1, 0), (2, 0), (1, 1), (2, 1)):
            codes, scales = weights[(d, b)]
            first = LEAD - d * RUN
            nc.tensor.matmul_mx(
                out=sums[b][:],
                lhsT=codes[:].bitcast(FP8X4),
                lhsT_scale=scales,
                rhs=x_codes[:, first : first + S].bitcast(FP8X4),
                rhs_scale=x_scales[:, first : first + S],
                start=(d == 0),
                stop=(d == TAPS - 1),
            )

        for b in range(BLOCKS):
            result = keep.tile([P, S], F32, name="result%d" % b)
            copy = nc.scalar.copy if b == 0 else nc.vector.tensor_copy
            copy(
                out=result[:].rearrange("p (i r) -> p i r", r=PHASES),
                in_=sums[b][:].rearrange("p (r i) -> p i r", r=PHASES),
            )
            nc.sync.dma_start(out=out[b * P : (b + 1) * P, :], in_=result[:])
